import numpy as np
import ml_dtypes


def mxq(x, axis, fmt="e4m3"):
    dtype, down = {"e4m3": (ml_dtypes.float8_e4m3fn, 7), "e5m2": (ml_dtypes.float8_e5m2, 14)}[fmt]
    v = np.moveaxis(np.asarray(x, np.float32).astype(ml_dtypes.bfloat16).astype(np.float64), axis, -1)
    blocks = v.reshape(v.shape[:-1] + (-1, 32))
    amax = np.abs(blocks).max(-1, keepdims=True)
    byte = np.maximum(np.where(amax > 0, np.frexp(amax)[1] - 1 + 127, 0) - down, 1)
    scale = np.exp2(byte - 127.0)
    codes = (blocks / scale).astype(np.float32).astype(dtype).astype(np.float64)
    return np.moveaxis((codes * scale).reshape(v.shape), -1, axis)


WIDE = False


def mx_kscale(k):
    if not WIDE:
        return np.ones(k)
    levels = np.array([10, -10, 5, -5, 0])
    if k % 512:
        return np.exp2(np.random.permutation(np.resize(levels, k // 32))).repeat(32)
    a = np.empty((k // 512, 16))
    for p in range(k // 512):
        a[p, :8] = np.random.permutation(np.resize(levels, 8))
        for g in range(8):
            far = levels[np.abs(levels - a[p, g]) >= 10]
            a[p, g + 8] = far[np.random.randint(len(far))]
    return np.exp2(a.ravel()).repeat(32)


def f64(x):
    return np.asarray(x).astype(np.float64)


def striped(idx):
    return np.tile(idx.reshape(-1, 16).T, (8, 1)).astype(np.uint16)


def unstriped(offs):
    return offs[:16].T.reshape(-1).astype(np.int64)


def pack_weight(w):
    k, n = w.shape
    w = f64(np.asarray(w, np.float32).astype(ml_dtypes.bfloat16)).reshape(k // 32, 32, n)
    amax = np.abs(w).max(1)
    byte = np.clip(np.where(amax > 0, np.frexp(amax)[1] - 1 + 127 - 7, 1), 1, 254)
    scaled = (w * np.exp2(127.0 - byte)[:, None, :]).reshape(k, n).astype(np.float32)
    words = np.ascontiguousarray(scaled.reshape(k // 512, 128, 4, n).transpose(0, 1, 3, 2)).astype(ml_dtypes.float8_e4m3fn).view(np.uint8)
    return words, np.ascontiguousarray(byte.astype(np.uint8).reshape(k // 512, 16, n))


def unpack_weight(words, scales):
    g, p, n, _ = words.shape
    vals = np.ascontiguousarray(words).view(ml_dtypes.float8_e4m3fn).astype(np.float64) * np.repeat(np.exp2(scales.astype(np.float64) - 127.0), 8, axis=1)[..., None]
    return vals.transpose(0, 1, 3, 2).reshape(g * 512, n)


K, T, S, H, W, C = 512, 2048, 512, 512, 384, 512


def setup_inputs():
    n = np.random.standard_normal
    s = mx_kscale(K)[:, None]
    packed_xT = pack_weight(n((K, T)) * s)
    return {
        "x_words": packed_xT[0],
        "x_scales": packed_xT[1],
        "w1": (n((K, H)) / np.sqrt(K) / s).astype(np.float32),
        "gs": (np.random.uniform(0.5, 1.5, (K, 1)) / s).astype(np.float32),
        "offs": striped(np.random.permutation(T)[:S]),
        "n1": striped(np.random.permutation(S)[:W]),
        "n2": striped(np.random.permutation(S)[:W]),
        "ca": striped(np.random.permutation(T)[:C]),
        "cb": striped(np.random.permutation(T)[:C]),
        "n3": striped(np.random.permutation(S)),
        "n4": striped(np.random.permutation(S)),
    }


def reference(x_words, x_scales, w1, gs, offs, n1, n2, ca, cb, n3, n4):
    x_ca = unpack_weight(x_words, x_scales)[:, unstriped(ca)]
    xq = unpack_weight(x_words, x_scales)[:, unstriped(offs)]
    y = mxq(f64(w1), 0, "e4m3").T @ xq
    old = y[:, unstriped(n1)]
    pa = y[:, unstriped(n2)]
    ra = old - np.tanh(pa)
    ds = y.copy()
    ds[:, unstriped(n1)] = ra
    z = f64(gs) * ds
    zq = mxq(z, 0, "e4m3")
    a = 0.0625 * (x_ca.T @ zq)
    x_cb = unpack_weight(x_words, x_scales)[:, unstriped(cb)]
    b = 0.0625 * (x_cb.T @ zq)
    return (a - a[:, unstriped(n3)]) / (np.abs(b) + np.abs(b[:, unstriped(n4)]) + 0.5)

@@ -1,0 +1,185 @@
+from contextlib import ExitStack
+
+import concourse.mybir as mybir
+
+K, T, S, H, W, C = 512, 2048, 512, 512, 384, 512
+FLOPS = 2 * K * H * S + 2 * 2 * H * C * S
+
+F32 = mybir.dt.float32
+BF16 = mybir.dt.bfloat16
+I32 = mybir.dt.int32
+U32 = mybir.dt.uint32
+U16 = mybir.dt.uint16
+U8 = mybir.dt.uint8
+FP8X4 = mybir.dt.float8_e4m3fn_x4
+ACT = mybir.ActivationFunctionType
+ALU = mybir.AluOpType
+
+P = 128
+PACK = 4
+HALF = S // 2
+
+
+def tile_picked_ccmpnormbktanh_none_p_kernel(tc, x_words, x_scales, w1, gs, offs, n1, n2, ca, cb, n3, n4, out):
+    nc = tc.nc
+    with ExitStack() as ctx:
+        keep = ctx.enter_context(tc.tile_pool(name="keep", bufs=1))
+        psum = ctx.enter_context(tc.psum_pool(name="psum", bufs=1))
+
+        def load_list(name, source):
+            tile = keep.tile(list(source.shape), U16, name=name)
+            nc.sync.dma_start(tile[:], source)
+            return tile
+
+        table_scales = keep.tile([P, T], U8, align_bytes=64)
+        nc.vector.memset(table_scales[:].bitcast(I32), 0)
+        w_raw = keep.tile([P, PACK, H], F32)
+        nc.sync.dma_start(out=w_raw[:], in_=w1.rearrange("(p j) h -> p j h", j=PACK))
+        for q in range(4):
+            nc.sync.dma_start(
+                out=table_scales[32 * q : 32 * q + 4, :].bitcast(I32),
+                in_=x_scales[0, 4 * q : 4 * q + 4, :].bitcast(I32),
+            )
+        offs_t = load_list("offs_t", offs)
+        table_words = keep.tile([P, T], U32, align_bytes=64)
+        nc.sync.dma_start(
+            out=table_words[:].bitcast(I32),
+            in_=x_words[0].rearrange("p n t -> p (n t)").bitcast(I32),
+        )
+        n1_t = load_list("n1_t", n1)
+        n2_t = load_list("n2_t", n2)
+        cb_t = load_list("cb_t", cb)
+        ca_t = load_list("ca_t", ca)
+        gain = keep.tile([P, PACK], F32)
+        nc.sync.dma_start(out=gain[:], in_=gs.rearrange("(p t) o -> p (t o)", t=PACK))
+        n4_t = load_list("n4_t", n4)
+        n3_t = load_list("n3_t", n3)
+
+        def gather_scales(name, offsets, tag):
+            tile = keep.tile([P, S], U8, name=name, tag=tag, align_bytes=64)
+            nc.vector.tensor_copy(tile[:], table_scales[:].indirect(offsets[:]))
+            return tile
+
+        def gather_words(name, offsets, tag):
+            tile = keep.tile([P, S], U32, name=name, tag=tag, align_bytes=64)
+            nc.vector.tensor_copy(tile[:], table_words[:].indirect(offsets[:]))
+            return tile
+
+        xq_scales = gather_scales("xq_scales", offs_t, "xq_scales")
+
+        w_codes, w_scales = [], []
+        w_view = w_raw[:].rearrange("p j (m t) -> p m j t", t=PACK)
+        for pair in range(2):
+            grouped = keep.tile([P, 2, P, PACK], BF16, name="w_grouped%d" % pair, align_bytes=64)
+            dst = grouped[:].rearrange("p t m j -> p m j t")
+            src = w_view[:, :, :, 2 * pair : 2 * pair + 2]
+            if pair == 0:
+                nc.vector.tensor_copy(out=dst, in_=src)
+            else:
+                nc.scalar.copy(out=dst, in_=src)
+            codes = keep.tile([P, 2 * P], U32, name="w_codes%d" % pair, align_bytes=64)
+            scales = keep.tile([P, 2 * P], U8, name="w_scales%d" % pair, align_bytes=64)
+            nc.vector.quantize_mx(
+                out=codes[:].bitcast(FP8X4),
+                scales=scales[:],
+                in_=grouped[:].rearrange("p t m j -> p (t m j)"),
+            )
+            w_codes.append(codes)
+            w_scales.append(scales)
+
+        xq_words = gather_words("xq_words", offs_t, "xq_words")
+
+        def product(bank, lhs_words, lhs_scales, rhs_words, rhs_scales):
+            acc = psum.tile([P, S], F32, name="acc", tag="bank%d" % bank)
+            nc.tensor.matmul_mx(
+                out=acc[:],
+                lhsT=lhs_words.bitcast(FP8X4),
+                lhsT_scale=lhs_scales,
+                rhs=rhs_words.bitcast(FP8X4),
+                rhs_scale=rhs_scales,
+                start=True,
+                stop=True,
+            )
+            return acc
+
+        y_acc = []
+        for t in range(PACK):
+            cols = slice((t % 2) * P, (t % 2 + 1) * P)
+            y_acc.append(product(t, w_codes[t // 2][:, cols], w_scales[t // 2][:, cols], xq_words[:], xq_scales[:]))
+
+        neg_tanh, y, old, ra = [], [], [], []
+        for t in range(PACK):
+            neg_tanh.append(keep.tile([P, S], F32, name="neg_tanh", tag="wide%d" % t, align_bytes=64))
+            nc.scalar.activation(neg_tanh[t][:], y_acc[t][:], ACT.Tanh, scale=-1.0)
+            y.append(keep.tile([P, S], F32, name="y%d" % t))
+            nc.vector.tensor_copy(out=y[t][:], in_=y_acc[t][:])
+        for t in range(PACK):
+            old.append(keep.tile([P, W], F32, name="old%d" % t))
+            nc.scalar.activation(old[t][:], y[t][:].indirect(n1_t[:]), ACT.Copy)
+            ra.append(keep.tile([P, W], F32, name="ra%d" % t))
+            nc.vector.tensor_tensor(ra[t][:], neg_tanh[t][:].indirect(n2_t[:]), old[t][:], ALU.add)
+        for t in range(PACK):
+            nc.scalar.activation(y[t][:].indirect(n1_t[:]), ra[t][:], ACT.Copy)
+        picked = {
+            "cb_words": gather_words("cb_words", cb_t, "wide0"),
+            "cb_scales": gather_scales("cb_scales", cb_t, "wide1"),
+            "ca_words": gather_words("ca_words", ca_t, "wide2"),
+            "ca_scales": gather_scales("ca_scales", ca_t, "wide3"),
+        }
+        z_grouped = keep.tile([P, S, PACK], BF16, align_bytes=64)
+        for t in range(PACK):
+            nc.vector.tensor_scalar(z_grouped[:, :, t], y[t][:], gain[:, t : t + 1], None, ALU.mult)
+
+        z_codes = keep.tile([P, S], U32, align_bytes=64)
+        z_scales = keep.tile([P, S], U8, align_bytes=64)
+        nc.vector.quantize_mx(
+            out=z_codes[:].bitcast(FP8X4),
+            scales=z_scales[:],
+            in_=z_grouped[:].rearrange("p s t -> p (s t)"),
+        )
+
+        halves = [(slice(h * HALF, (h + 1) * HALF), slice(h * HALF // 16, (h + 1) * HALF // 16)) for h in range(2)]
+        tiles = C // P
+        b_acc, a_acc = [], []
+        for c in range(tiles):
+            rows = slice(c * P, (c + 1) * P)
+            b_acc.append(product((4 + 2 * c) % 8, picked["cb_words"][:, rows], picked["cb_scales"][:, rows], z_codes[:], z_scales[:]))
+            a_acc.append(product((5 + 2 * c) % 8, picked["ca_words"][:, rows], picked["ca_scales"][:, rows], z_codes[:], z_scales[:]))
+
+        b_sizes = []
+        for c in range(tiles):
+            b_sizes.append(keep.tile([P, S], F32, name="b_size%d" % c))
+            nc.scalar.activation(b_sizes[c][:], b_acc[c][:], ACT.Abs)
+
+        def look_up(c):
+            b_size = b_sizes[c]
+            a = keep.tile([P, S], F32, name="a%d" % c)
+            if c + 1 < tiles:
+                nc.vector.tensor_copy(out=a[:], in_=a_acc[c][:])
+            else:
+                nc.scalar.copy(out=a[:], in_=a_acc[c][:])
+            b_plus = keep.tile([P, S], F32, name="b_plus%d" % c)
+            nc.vector.tensor_scalar(b_plus[:], b_size[:], 8.0, None, ALU.add)
+            a_other = keep.tile([P, S], F32, name="a_other%d" % c)
+            denom = keep.tile([P, S], F32, name="denom%d" % c)
+            for cols, entries in halves:
+                nc.scalar.activation(a_other[:, cols], a[:].indirect(n3_t[:, entries]), ACT.Copy)
+                nc.vector.tensor_tensor(denom[:, cols], b_size[:].indirect(n4_t[:, entries]), b_plus[:, cols], ALU.add)
+            return a, a_other, denom
+
+        def finish(c, a, a_other, denom):
+            root = keep.tile([P, S], F32, name="root%d" % c)
+            nc.scalar.activation(root[:], denom[:], ACT.Abs_reciprocal_sqrt)
+            inverse = keep.tile([P, S], F32, name="inverse%d" % c)
+            nc.scalar.activation(inverse[:], root[:], ACT.Square)
+            numer = keep.tile([P, S], F32, name="numer%d" % c)
+            nc.vector.tensor_tensor(numer[:], a[:], a_other[:], ALU.subtract)
+            result = keep.tile([P, S], F32, name="result%d" % c)
+            nc.vector.tensor_tensor(result[:], numer[:], inverse[:], ALU.mult)
+            nc.sync.dma_start(out=out[c * P : (c + 1) * P, :], in_=result[:])
+
+        looked = [look_up(0), look_up(1)]
+        for c in range(tiles):
+            if c + 2 < tiles:
+                looked.append(look_up(c + 2))
+            finish(c, *looked[c])

@@ -87,10 +87,14 @@ def tile_picked_ccmpnormbktanh_none_p_kernel(tc, x_words, x_scales, w1, gs, offs
             w_codes.append(codes)
             w_scales.append(scales)
 
-        xq_words = gather_words("xq_words", offs_t, "xq_words")
+        halves = [(slice(h * HALF, (h + 1) * HALF), slice(h * HALF // 16, (h + 1) * HALF // 16)) for h in range(2)]
+        xq_words = []
+        for h, (cols, entries) in enumerate(halves):
+            xq_words.append(keep.tile([P, HALF], U32, name="xq_words%d" % h, align_bytes=64))
+            nc.vector.tensor_copy(xq_words[h][:], table_words[:].indirect(offs_t[:, entries]))
 
-        def product(bank, lhs_words, lhs_scales, rhs_words, rhs_scales):
-            acc = psum.tile([P, S], F32, name="acc", tag="bank%d" % bank)
+        def product(bank, width, lhs_words, lhs_scales, rhs_words, rhs_scales):
+            acc = psum.tile([P, width], F32, name="acc", tag="bank%d" % bank)
             nc.tensor.matmul_mx(
                 out=acc[:],
                 lhsT=lhs_words.bitcast(FP8X4),
@@ -102,17 +106,17 @@ def tile_picked_ccmpnormbktanh_none_p_kernel(tc, x_words, x_scales, w1, gs, offs
             )
             return acc
 
-        y_acc = []
-        for t in range(PACK):
-            cols = slice((t % 2) * P, (t % 2 + 1) * P)
-            y_acc.append(product(t, w_codes[t // 2][:, cols], w_scales[t // 2][:, cols], xq_words[:], xq_scales[:]))
-
-        neg_tanh, y, old, ra = [], [], [], []
-        for t in range(PACK):
-            neg_tanh.append(keep.tile([P, S], F32, name="neg_tanh", tag="wide%d" % t, align_bytes=64))
-            nc.scalar.activation(neg_tanh[t][:], y_acc[t][:], ACT.Tanh, scale=-1.0)
-            y.append(keep.tile([P, S], F32, name="y%d" % t))
-            nc.vector.tensor_copy(out=y[t][:], in_=y_acc[t][:])
+        neg_tanh = [keep.tile([P, S], F32, name="neg_tanh", tag="wide%d" % t, align_bytes=64) for t in range(PACK)]
+        y = [keep.tile([P, S], F32, name="y%d" % t) for t in range(PACK)]
+        for pair in range(2):
+            for h, (cols, entries) in enumerate(halves):
+                for u in range(2):
+                    t = 2 * pair + u
+                    w_cols = slice(u * P, (u + 1) * P)
+                    acc = product(2 * t + h, HALF, w_codes[pair][:, w_cols], w_scales[pair][:, w_cols], xq_words[h][:], xq_scales[:, cols])
+                    nc.scalar.activation(neg_tanh[t][:, cols], acc[:], ACT.Tanh, scale=-1.0)
+                    nc.vector.tensor_copy(out=y[t][:, cols], in_=acc[:])
+        old, ra = [], []
         for t in range(PACK):
             old.append(keep.tile([P, W], F32, name="old%d" % t))
             nc.scalar.activation(old[t][:], y[t][:].indirect(n1_t[:]), ACT.Copy)
@@ -126,60 +130,63 @@ def tile_picked_ccmpnormbktanh_none_p_kernel(tc, x_words, x_scales, w1, gs, offs
             "ca_words": gather_words("ca_words", ca_t, "wide2"),
             "ca_scales": gather_scales("ca_scales", ca_t, "wide3"),
         }
-        z_grouped = keep.tile([P, S, PACK], BF16, align_bytes=64)
+        z_grouped = [keep.tile([P, HALF, PACK], BF16, name="z_grouped%d" % h, align_bytes=64) for h in range(2)]
         for t in range(PACK):
-            nc.vector.tensor_scalar(z_grouped[:, :, t], y[t][:], gain[:, t : t + 1], None, ALU.mult)
+            for h, (cols, entries) in enumerate(halves):
+                nc.vector.tensor_scalar(z_grouped[h][:, :, t], y[t][:, cols], gain[:, t : t + 1], None, ALU.mult)
 
         z_codes = keep.tile([P, S], U32, align_bytes=64)
         z_scales = keep.tile([P, S], U8, align_bytes=64)
-        nc.vector.quantize_mx(
-            out=z_codes[:].bitcast(FP8X4),
-            scales=z_scales[:],
-            in_=z_grouped[:].rearrange("p s t -> p (s t)"),
-        )
+        for h, (cols, entries) in enumerate(halves):
+            nc.vector.quantize_mx(
+                out=z_codes[:, cols].bitcast(FP8X4),
+                scales=z_scales[:, cols],
+                in_=z_grouped[h][:].rearrange("p s t -> p (s t)"),
+            )
 
-        halves = [(slice(h * HALF, (h + 1) * HALF), slice(h * HALF // 16, (h + 1) * HALF // 16)) for h in range(2)]
         tiles = C // P
-        b_acc, a_acc = [], []
+        b_size = [keep.tile([P, S], F32, name="b_size%d" % c) for c in range(tiles)]
+        b_twin = [keep.tile([P, S], F32, name="b_twin%d" % c) for c in range(tiles)]
+        for h, (cols, entries) in enumerate(halves):
+            acc = product(h, HALF, picked["cb_words"][:, 0:P], picked["cb_scales"][:, 0:P], z_codes[:, cols], z_scales[:, cols])
+            nc.scalar.activation(b_size[0][:, cols], acc[:], ACT.Abs)
+        nc.vector.tensor_copy(out=b_twin[0][:], in_=b_size[0][:])
+        for c in range(1, tiles):
+            rows = slice(c * P, (c + 1) * P)
+            acc = product(1 + c, S, picked["cb_words"][:, rows], picked["cb_scales"][:, rows], z_codes[:], z_scales[:])
+            nc.scalar.activation(b_size[c][:], acc[:], ACT.Abs)
+            nc.sync.dma_start(out=b_twin[c][:], in_=b_size[c][:])
+        a_acc = []
         for c in range(tiles):
             rows = slice(c * P, (c + 1) * P)
-            b_acc.append(product((4 + 2 * c) % 8, picked["cb_words"][:, rows], picked["cb_scales"][:, rows], z_codes[:], z_scales[:]))
-            a_acc.append(product((5 + 2 * c) % 8, picked["ca_words"][:, rows], picked["ca_scales"][:, rows], z_codes[:], z_scales[:]))
-
-        b_sizes = []
-        for c in range(tiles):
-            b_sizes.append(keep.tile([P, S], F32, name="b_size%d" % c))
-            nc.scalar.activation(b_sizes[c][:], b_acc[c][:], ACT.Abs)
+            a_acc.append(product((5 + c) % 8, S, picked["ca_words"][:, rows], picked["ca_scales"][:, rows], z_codes[:], z_scales[:]))
 
         def look_up(c):
-            b_size = b_sizes[c]
-            a = keep.tile([P, S], F32, name="a%d" % c)
-            if c + 1 < tiles:
-                nc.vector.tensor_copy(out=a[:], in_=a_acc[c][:])
-            else:
-                nc.scalar.copy(out=a[:], in_=a_acc[c][:])
-            b_plus = keep.tile([P, S], F32, name="b_plus%d" % c)
-            nc.vector.tensor_scalar(b_plus[:], b_size[:], 8.0, None, ALU.add)
-            a_other = keep.tile([P, S], F32, name="a_other%d" % c)
             denom = keep.tile([P, S], F32, name="denom%d" % c)
             for cols, entries in halves:
+                nc.vector.tensor_tensor(denom[:, cols], b_size[c][:].indirect(n4_t[:, entries]), b_twin[c][:, cols], ALU.add)
+            a = keep.tile([P, S], F32, name="a%d" % c)
+            nc.vector.tensor_copy(out=a[:], in_=a_acc[c][:])
+            a_other = keep.tile([P, S], F32, name="a_other%d" % c)
+            for cols, entries in halves:
                 nc.scalar.activation(a_other[:, cols], a[:].indirect(n3_t[:, entries]), ACT.Copy)
-                nc.vector.tensor_tensor(denom[:, cols], b_size[:].indirect(n4_t[:, entries]), b_plus[:, cols], ALU.add)
-            return a, a_other, denom
-
-        def finish(c, a, a_other, denom):
             root = keep.tile([P, S], F32, name="root%d" % c)
-            nc.scalar.activation(root[:], denom[:], ACT.Abs_reciprocal_sqrt)
+            nc.scalar.activation(root[:], denom[:], ACT.Abs_reciprocal_sqrt, bias=8.0)
             inverse = keep.tile([P, S], F32, name="inverse%d" % c)
             nc.scalar.activation(inverse[:], root[:], ACT.Square)
-            numer = keep.tile([P, S], F32, name="numer%d" % c)
-            nc.vector.tensor_tensor(numer[:], a[:], a_other[:], ALU.subtract)
-            result = keep.tile([P, S], F32, name="result%d" % c)
-            nc.vector.tensor_tensor(result[:], numer[:], inverse[:], ALU.mult)
-            nc.sync.dma_start(out=out[c * P : (c + 1) * P, :], in_=result[:])
+            return a, a_other, inverse
 
-        looked = [look_up(0), look_up(1)]
+        def finish(c, a, a_other, inverse):
+            numer = keep.tile([P, S], F32, name="numer%d" % c)
+            result = keep.tile([P, S], F32, name="result%d" % c)
+            pieces = [cols for cols, entries in halves] if c == tiles - 1 else [slice(0, S)]
+            for cols in pieces:
+                nc.vector.tensor_tensor(numer[:, cols], a[:, cols], a_other[:, cols], ALU.subtract)
+                nc.vector.tensor_tensor(result[:, cols], numer[:, cols], inverse[:, cols], ALU.mult)
+                nc.sync.dma_start(out=out[c * P : (c + 1) * P, cols], in_=result[:, cols])
+
+        looked = [look_up(0)]
         for c in range(tiles):
-            if c + 2 < tiles:
-                looked.append(look_up(c + 2))
+            if c + 1 < tiles:
+                looked.append(look_up(c + 1))
             finish(c, *looked[c])

@@ -128,9 +128,10 @@ def tile_picked_ccmpnormbktanh_none_p_kernel(tc, x_words, x_scales, w1, gs, offs
             "cb_words": gather_words("cb_words", cb_t, "wide0"),
             "cb_scales": gather_scales("cb_scales", cb_t, "wide1"),
             "ca_words": gather_words("ca_words", ca_t, "wide2"),
-            "ca_scales": gather_scales("ca_scales", ca_t, "wide3"),
         }
-        z_grouped = [keep.tile([P, HALF, PACK], BF16, name="z_grouped%d" % h, align_bytes=64) for h in range(2)]
+        table_warm = keep.tile([P, 1], F32)
+        nc.scalar.activation(table_warm[:], y[PACK - 1][:, 0:1], ACT.Abs_reciprocal_sqrt, bias=8.0, scale=0.0)
+        z_grouped = [keep.tile([P, HALF, PACK], BF16, name="z_grouped", tag="grouped%d" % h, align_bytes=64) for h in range(2)]
         for t in range(PACK):
             for h, (cols, entries) in enumerate(halves):
                 nc.vector.tensor_scalar(z_grouped[h][:, :, t], y[t][:, cols], gain[:, t : t + 1], None, ALU.mult)
@@ -143,6 +144,8 @@ def tile_picked_ccmpnormbktanh_none_p_kernel(tc, x_words, x_scales, w1, gs, offs
                 scales=z_scales[:, cols],
                 in_=z_grouped[h][:].rearrange("p s t -> p (s t)"),
             )
+
+        picked["ca_scales"] = gather_scales("ca_scales", ca_t, "grouped1")
 
         tiles = C // P
         b_size = [keep.tile([P, S], F32, name="b_size%d" % c) for c in range(tiles)]
@@ -161,26 +164,32 @@ def tile_picked_ccmpnormbktanh_none_p_kernel(tc, x_words, x_scales, w1, gs, offs
             rows = slice(c * P, (c + 1) * P)
             a_acc.append(product((5 + c) % 8, S, picked["ca_words"][:, rows], picked["ca_scales"][:, rows], z_codes[:], z_scales[:]))
 
+        def pieces(c):
+            return [cols for cols, entries in halves] if c == tiles - 1 else [slice(0, S)]
+
         def look_up(c):
             denom = keep.tile([P, S], F32, name="denom%d" % c)
             for cols, entries in halves:
                 nc.vector.tensor_tensor(denom[:, cols], b_size[c][:].indirect(n4_t[:, entries]), b_twin[c][:, cols], ALU.add)
             a = keep.tile([P, S], F32, name="a%d" % c)
-            nc.vector.tensor_copy(out=a[:], in_=a_acc[c][:])
+            if c < 2:
+                nc.scalar.copy(out=a[:], in_=a_acc[c][:])
+            else:
+                nc.vector.tensor_copy(out=a[:], in_=a_acc[c][:])
             a_other = keep.tile([P, S], F32, name="a_other%d" % c)
             for cols, entries in halves:
                 nc.scalar.activation(a_other[:, cols], a[:].indirect(n3_t[:, entries]), ACT.Copy)
             root = keep.tile([P, S], F32, name="root%d" % c)
-            nc.scalar.activation(root[:], denom[:], ACT.Abs_reciprocal_sqrt, bias=8.0)
             inverse = keep.tile([P, S], F32, name="inverse%d" % c)
-            nc.scalar.activation(inverse[:], root[:], ACT.Square)
+            for cols in pieces(c):
+                nc.scalar.activation(root[:, cols], denom[:, cols], ACT.Abs_reciprocal_sqrt, bias=8.0)
+                nc.scalar.activation(inverse[:, cols], root[:, cols], ACT.Square)
             return a, a_other, inverse
 
         def finish(c, a, a_other, inverse):
             numer = keep.tile([P, S], F32, name="numer%d" % c)
             result = keep.tile([P, S], F32, name="result%d" % c)
-            pieces = [cols for cols, entries in halves] if c == tiles - 1 else [slice(0, S)]
-            for cols in pieces:
+            for cols in pieces(c):
                 nc.vector.tensor_tensor(numer[:, cols], a[:, cols], a_other[:, cols], ALU.subtract)
                 nc.vector.tensor_tensor(result[:, cols], numer[:, cols], inverse[:, cols], ALU.mult)
                 nc.sync.dma_start(out=out[c * P : (c + 1) * P, cols], in_=result[:, cols])

from contextlib import ExitStack

import concourse.mybir as mybir

K, T, S, H, W, C = 512, 2048, 512, 512, 384, 512
FLOPS = 2 * K * H * S + 2 * 2 * H * C * S

F32 = mybir.dt.float32
BF16 = mybir.dt.bfloat16
I32 = mybir.dt.int32
U32 = mybir.dt.uint32
U16 = mybir.dt.uint16
U8 = mybir.dt.uint8
FP8X4 = mybir.dt.float8_e4m3fn_x4
ACT = mybir.ActivationFunctionType
ALU = mybir.AluOpType

P = 128
PACK = 4
HALF = S // 2


def tile_picked_ccmpnormbktanh_none_p_kernel(tc, x_words, x_scales, w1, gs, offs, n1, n2, ca, cb, n3, n4, out):
    nc = tc.nc
    with ExitStack() as ctx:
        keep = ctx.enter_context(tc.tile_pool(name="keep", bufs=1))
        psum = ctx.enter_context(tc.psum_pool(name="psum", bufs=1))

        def load_list(name, source):
            tile = keep.tile(list(source.shape), U16, name=name)
            nc.sync.dma_start(tile[:], source)
            return tile

        table_scales = keep.tile([P, T], U8, align_bytes=64)
        nc.vector.memset(table_scales[:].bitcast(I32), 0)
        w_raw = keep.tile([P, PACK, H], F32)
        nc.sync.dma_start(out=w_raw[:], in_=w1.rearrange("(p j) h -> p j h", j=PACK))
        for q in range(4):
            nc.sync.dma_start(
                out=table_scales[32 * q : 32 * q + 4, :].bitcast(I32),
                in_=x_scales[0, 4 * q : 4 * q + 4, :].bitcast(I32),
            )
        offs_t = load_list("offs_t", offs)
        table_words = keep.tile([P, T], U32, align_bytes=64)
        nc.sync.dma_start(
            out=table_words[:].bitcast(I32),
            in_=x_words[0].rearrange("p n t -> p (n t)").bitcast(I32),
        )
        n1_t = load_list("n1_t", n1)
        n2_t = load_list("n2_t", n2)
        cb_t = load_list("cb_t", cb)
        ca_t = load_list("ca_t", ca)
        gain = keep.tile([P, PACK], F32)
        nc.sync.dma_start(out=gain[:], in_=gs.rearrange("(p t) o -> p (t o)", t=PACK))
        n4_t = load_list("n4_t", n4)
        n3_t = load_list("n3_t", n3)

        def gather_scales(name, offsets, tag):
            tile = keep.tile([P, S], U8, name=name, tag=tag, align_bytes=64)
            nc.vector.tensor_copy(tile[:], table_scales[:].indirect(offsets[:]))
            return tile

        def gather_words(name, offsets, tag):
            tile = keep.tile([P, S], U32, name=name, tag=tag, align_bytes=64)
            nc.vector.tensor_copy(tile[:], table_words[:].indirect(offsets[:]))
            return tile

        xq_scales = gather_scales("xq_scales", offs_t, "xq_scales")

        w_codes, w_scales = [], []
        w_view = w_raw[:].rearrange("p j (m t) -> p m j t", t=PACK)
        for pair in range(2):
            grouped = keep.tile([P, 2, P, PACK], BF16, name="w_grouped%d" % pair, align_bytes=64)
            dst = grouped[:].rearrange("p t m j -> p m j t")
            src = w_view[:, :, :, 2 * pair : 2 * pair + 2]
            if pair == 0:
                nc.vector.tensor_copy(out=dst, in_=src)
            else:
                nc.scalar.copy(out=dst, in_=src)
            codes = keep.tile([P, 2 * P], U32, name="w_codes%d" % pair, align_bytes=64)
            scales = keep.tile([P, 2 * P], U8, name="w_scales%d" % pair, align_bytes=64)
            nc.vector.quantize_mx(
                out=codes[:].bitcast(FP8X4),
                scales=scales[:],
                in_=grouped[:].rearrange("p t m j -> p (t m j)"),
            )
            w_codes.append(codes)
            w_scales.append(scales)

        halves = [(slice(h * HALF, (h + 1) * HALF), slice(h * HALF // 16, (h + 1) * HALF // 16)) for h in range(2)]
        xq_words = []
        for h, (cols, entries) in enumerate(halves):
            xq_words.append(keep.tile([P, HALF], U32, name="xq_words%d" % h, align_bytes=64))
            nc.vector.tensor_copy(xq_words[h][:], table_words[:].indirect(offs_t[:, entries]))

        def product(bank, width, lhs_words, lhs_scales, rhs_words, rhs_scales):
            acc = psum.tile([P, width], F32, name="acc", tag="bank%d" % bank)
            nc.tensor.matmul_mx(
                out=acc[:],
                lhsT=lhs_words.bitcast(FP8X4),
                lhsT_scale=lhs_scales,
                rhs=rhs_words.bitcast(FP8X4),
                rhs_scale=rhs_scales,
                start=True,
                stop=True,
            )
            return acc

        neg_tanh = [keep.tile([P, S], F32, name="neg_tanh", tag="wide%d" % t, align_bytes=64) for t in range(PACK)]
        y = [keep.tile([P, S], F32, name="y%d" % t) for t in range(PACK)]
        for pair in range(2):
            for h, (cols, entries) in enumerate(halves):
                for u in range(2):
                    t = 2 * pair + u
                    w_cols = slice(u * P, (u + 1) * P)
                    acc = product(2 * t + h, HALF, w_codes[pair][:, w_cols], w_scales[pair][:, w_cols], xq_words[h][:], xq_scales[:, cols])
                    nc.scalar.activation(neg_tanh[t][:, cols], acc[:], ACT.Tanh, scale=-1.0)
                    nc.vector.tensor_copy(out=y[t][:, cols], in_=acc[:])
        old, ra = [], []
        for t in range(PACK):
            old.append(keep.tile([P, W], F32, name="old%d" % t))
            nc.scalar.activation(old[t][:], y[t][:].indirect(n1_t[:]), ACT.Copy)
            ra.append(keep.tile([P, W], F32, name="ra%d" % t))
            nc.vector.tensor_tensor(ra[t][:], neg_tanh[t][:].indirect(n2_t[:]), old[t][:], ALU.add)
        for t in range(PACK):
            nc.scalar.activation(y[t][:].indirect(n1_t[:]), ra[t][:], ACT.Copy)
        picked = {
            "cb_words": gather_words("cb_words", cb_t, "wide0"),
            "cb_scales": gather_scales("cb_scales", cb_t, "wide1"),
            "ca_words": gather_words("ca_words", ca_t, "wide2"),
        }
        table_warm = keep.tile([P, 1], F32)
        nc.scalar.activation(table_warm[:], y[PACK - 1][:, 0:1], ACT.Abs_reciprocal_sqrt, bias=8.0, scale=0.0)
        z_grouped = [keep.tile([P, HALF, PACK], BF16, name="z_grouped", tag="grouped%d" % h, align_bytes=64) for h in range(2)]
        for t in range(PACK):
            for h, (cols, entries) in enumerate(halves):
                nc.vector.tensor_scalar(z_grouped[h][:, :, t], y[t][:, cols], gain[:, t : t + 1], None, ALU.mult)

        z_codes = keep.tile([P, S], U32, align_bytes=64)
        z_scales = keep.tile([P, S], U8, align_bytes=64)
        for h, (cols, entries) in enumerate(halves):
            nc.vector.quantize_mx(
                out=z_codes[:, cols].bitcast(FP8X4),
                scales=z_scales[:, cols],
                in_=z_grouped[h][:].rearrange("p s t -> p (s t)"),
            )

        picked["ca_scales"] = gather_scales("ca_scales", ca_t, "grouped1")

        tiles = C // P
        b_size = [keep.tile([P, S], F32, name="b_size%d" % c) for c in range(tiles)]
        b_twin = [keep.tile([P, S], F32, name="b_twin%d" % c) for c in range(tiles)]
        for h, (cols, entries) in enumerate(halves):
            acc = product(h, HALF, picked["cb_words"][:, 0:P], picked["cb_scales"][:, 0:P], z_codes[:, cols], z_scales[:, cols])
            nc.scalar.activation(b_size[0][:, cols], acc[:], ACT.Abs)
        nc.vector.tensor_copy(out=b_twin[0][:], in_=b_size[0][:])
        for c in range(1, tiles):
            rows = slice(c * P, (c + 1) * P)
            acc = product(1 + c, S, picked["cb_words"][:, rows], picked["cb_scales"][:, rows], z_codes[:], z_scales[:])
            nc.scalar.activation(b_size[c][:], acc[:], ACT.Abs)
            nc.sync.dma_start(out=b_twin[c][:], in_=b_size[c][:])
        a_acc = []
        for c in range(tiles):
            rows = slice(c * P, (c + 1) * P)
            a_acc.append(product((5 + c) % 8, S, picked["ca_words"][:, rows], picked["ca_scales"][:, rows], z_codes[:], z_scales[:]))

        def pieces(c):
            return [cols for cols, entries in halves] if c == tiles - 1 else [slice(0, S)]

        def look_up(c):
            denom = keep.tile([P, S], F32, name="denom%d" % c)
            for cols, entries in halves:
                nc.vector.tensor_tensor(denom[:, cols], b_size[c][:].indirect(n4_t[:, entries]), b_twin[c][:, cols], ALU.add)
            a = keep.tile([P, S], F32, name="a%d" % c)
            if c < 2:
                nc.scalar.copy(out=a[:], in_=a_acc[c][:])
            else:
                nc.vector.tensor_copy(out=a[:], in_=a_acc[c][:])
            a_other = keep.tile([P, S], F32, name="a_other%d" % c)
            for cols, entries in halves:
                nc.scalar.activation(a_other[:, cols], a[:].indirect(n3_t[:, entries]), ACT.Copy)
            root = keep.tile([P, S], F32, name="root%d" % c)
            inverse = keep.tile([P, S], F32, name="inverse%d" % c)
            for cols in pieces(c):
                nc.scalar.activation(root[:, cols], denom[:, cols], ACT.Abs_reciprocal_sqrt, bias=8.0)
                nc.scalar.activation(inverse[:, cols], root[:, cols], ACT.Square)
            return a, a_other, inverse

        def finish(c, a, a_other, inverse):
            numer = keep.tile([P, S], F32, name="numer%d" % c)
            result = keep.tile([P, S], F32, name="result%d" % c)
            for cols in pieces(c):
                nc.vector.tensor_tensor(numer[:, cols], a[:, cols], a_other[:, cols], ALU.subtract)
                nc.vector.tensor_tensor(result[:, cols], numer[:, cols], inverse[:, cols], ALU.mult)
                nc.sync.dma_start(out=out[c * P : (c + 1) * P, cols], in_=result[:, cols])

        looked = [look_up(0)]
        for c in range(tiles):
            if c + 1 < tiles:
                looked.append(look_up(c + 1))
            finish(c, *looked[c])
